import numpy as np
import ml_dtypes


def mxq(x, axis, fmt="e4m3"):
    dtype, down = {"e4m3": (ml_dtypes.float8_e4m3fn, 7), "e5m2": (ml_dtypes.float8_e5m2, 14)}[fmt]
    v = np.moveaxis(np.asarray(x, np.float32).astype(ml_dtypes.bfloat16).astype(np.float64), axis, -1)
    blocks = v.reshape(v.shape[:-1] + (-1, 32))
    amax = np.abs(blocks).max(-1, keepdims=True)
    byte = np.maximum(np.where(amax > 0, np.frexp(amax)[1] - 1 + 127, 0) - down, 1)
    scale = np.exp2(byte - 127.0)
    codes = (blocks / scale).astype(np.float32).astype(dtype).astype(np.float64)
    return np.moveaxis((codes * scale).reshape(v.shape), -1, axis)


WIDE = False


def mx_kscale(k):
    if not WIDE:
        return np.ones(k)
    levels = np.array([10, -10, 5, -5, 0])
    if k % 512:
        return np.exp2(np.random.permutation(np.resize(levels, k // 32))).repeat(32)
    a = np.empty((k // 512, 16))
    for p in range(k // 512):
        a[p, :8] = np.random.permutation(np.resize(levels, 8))
        for g in range(8):
            far = levels[np.abs(levels - a[p, g]) >= 10]
            a[p, g + 8] = far[np.random.randint(len(far))]
    return np.exp2(a.ravel()).repeat(32)


BF16 = ml_dtypes.bfloat16


def bf(x):
    return np.asarray(x, np.float32).astype(BF16)


def f64(x):
    return np.asarray(x).astype(np.float64)


E2M1 = np.array([0.0, 0.5, 1.0, 1.5, 2.0, 3.0, 4.0, 6.0, -0.0, -0.5, -1.0, -1.5, -2.0, -3.0, -4.0, -6.0])


def pack_weight(w, fmt):
    k, n = w.shape
    w = f64(bf(w)).reshape(k // 32, 32, n)
    amax = np.abs(w).max(1)
    if fmt == "e4m3":
        byte = np.frexp(amax)[1] - 1 + 127 - 7
    else:
        mant, ex = np.frexp(amax / 6.0)
        byte = np.where(mant > 0.5, ex, ex - 1) + 127
    byte = np.clip(np.where(amax > 0, byte, 1), 1, 254)
    scaled = (w * np.exp2(127.0 - byte)[:, None, :]).reshape(k, n).astype(np.float32)
    by_word = np.ascontiguousarray(scaled.reshape(k // 512, 128, 4, n).transpose(0, 1, 3, 2))
    if fmt == "e4m3":
        words = by_word.astype(ml_dtypes.float8_e4m3fn).view(np.uint8)
    else:
        c = by_word.astype(ml_dtypes.float4_e2m1fn).view(np.uint8) & 0xF
        words = c[..., 0::2] | (c[..., 1::2] << 4)
    return np.ascontiguousarray(words), np.ascontiguousarray(byte.astype(np.uint8).reshape(k // 512, 16, n))


def unpack_weight(words, scales, fmt):
    g, p, n, _ = words.shape
    if fmt == "e4m3":
        vals = np.ascontiguousarray(words).view(ml_dtypes.float8_e4m3fn).astype(np.float64)
    else:
        nib = np.empty((g, p, n, 4), np.uint8)
        nib[..., 0::2] = words & 0xF
        nib[..., 1::2] = words >> 4
        vals = E2M1[nib]
    vals = vals * np.repeat(np.exp2(scales.astype(np.float64) - 127.0), 8, axis=1)[..., None]
    return vals.transpose(0, 1, 3, 2).reshape(g * 512, n)
def pack4(w):
    words, scales = pack_weight(w, "e2m1")
    return words.reshape(words.shape[0], 128, -1), scales


def unpack4(words, scales):
    return unpack_weight(words.reshape(words.shape[0], 128, -1, 2), scales, "e2m1")


def planes(Y):
    n, m = Y.shape
    b = f64(bf(Y)).reshape(n // 32, 32, m)
    amax = np.abs(b).max(1)
    byte = np.clip(np.where(amax > 0, np.frexp(amax)[1] - 1 + 127 - 7, 1), 1, 254)
    codes = (b * np.exp2(127.0 - byte)[:, None, :]).reshape(n, m).astype(np.float32).astype(ml_dtypes.float8_e4m3fn).view(np.uint8)
    words = codes.reshape(n // 512, 128, 4, m).transpose(0, 1, 3, 2)
    return np.ascontiguousarray(words), np.ascontiguousarray(byte.astype(np.uint8).reshape(n // 512, 16, m))


S, G, V, L = 1024, 1024, 1536, 6
SHARED = 0.8
WEIGHT = 0.08

def unit_columns(z):
    z = z - z.mean(axis=0)
    return z / np.sqrt((z * z).sum(axis=0))

def along_axes(axes, load):
    return unit_columns((axes[:, :, None] * load[None, :, :]).sum(axis=1))

def noisy(z):
    return np.sqrt(SHARED * S) * z + np.sqrt(1.0 - SHARED) * np.random.randn(*z.shape)

def called_dosages(truth, offset):
    return unit_columns(2.0 / (1.0 + np.exp(-(offset + noisy(truth)))))

def setup_inputs():
    s = mx_kscale(S)[:, None]
    axes = np.random.randn(S, L)
    expression = unit_columns(noisy(along_axes(axes, np.random.randn(L, G))))
    truth = along_axes(axes, np.random.randn(L, V))
    offset = 0.5 * np.random.randn(V)
    c = np.sqrt(S - 2.0) * WEIGHT * np.exp(0.8 * np.random.randn(V))
    x_words, x_scales = pack_weight(expression * s, "e4m3")
    a_words, a_scales = pack4(called_dosages(truth, offset) / s)
    b_words, b_scales = pack_weight(called_dosages(truth, offset) / s, "e4m3")
    u = bf(called_dosages(truth, offset) * c / s)
    return {"x_words": x_words, "x_scales": x_scales, "a_words": a_words, "a_scales": a_scales,
            "b_words": b_words, "b_scales": b_scales, "u": u}

def reference(x_words, x_scales, a_words, a_scales, b_words, b_scales, u):
    xt = unpack_weight(x_words, x_scales, "e4m3").T
    ra = xt @ unpack4(a_words, a_scales)
    rb = xt @ unpack_weight(b_words, b_scales, "e4m3")
    ru = xt @ mxq(f64(u), 0, "e4m3")
    y = ru / np.sqrt(1.0 - ra * rb)
    Y = y.T
    words, scales = planes(Y)
    return y, words, scales

@@ -1,0 +1,302 @@
+from contextlib import ExitStack
+
+import concourse.mybir as mybir
+from concourse.masks import make_identity
+
+S, G, V = 1024, 1024, 1536
+FLOPS = 3 * 2 * S * G * V
+
+F32 = mybir.dt.float32
+BF16 = mybir.dt.bfloat16
+I32 = mybir.dt.int32
+U32 = mybir.dt.uint32
+U8 = mybir.dt.uint8
+FP8X4 = mybir.dt.float8_e4m3fn_x4
+FP4X4 = mybir.dt.float4_e2m1fn_x4
+ALU = mybir.AluOpType
+ACT = mybir.ActivationFunctionType
+
+P = 128
+PACK = 4
+K_PASS = P * PACK
+PASSES = S // K_PASS
+CHUNK = 512
+CHUNKS = V // CHUNK
+GENE_TILES = G // P
+TILES = CHUNKS * GENE_TILES
+
+FIRST_LAG = 9
+DOUBLE_STEPS = (10, 13, 16, 19, 22)
+POOL_CASTS = True
+RS_LAG = 2
+TR_LAG = 3
+TC_LAG = 0
+QY_LAG = 2
+HEAD = (4, 6, 6, 8)
+U_FIRST = (9, 15)
+U_ENG = "SSSV"
+WARM = 0
+
+
+def program_order():
+    ru_step = []
+    n = FIRST_LAG
+    while len(ru_step) < TILES:
+        ru_step.append(n)
+        if n in DOUBLE_STEPS and len(ru_step) < TILES:
+            ru_step.append(n)
+        n += 1
+    end = ru_step[-1]
+    groups = []
+    for j in range(5):
+        ts = ru_step[4 * j + 3] + TR_LAG
+        groups.append(((4 * j, 4 * j + 1), ts, ts + TC_LAG, ts + QY_LAG))
+        groups.append(((4 * j + 2, 4 * j + 3), ts, ts + TC_LAG, None))
+    groups.append(((20, 21), end + 1, end + 1, end + 2))
+    groups.append(((22,), end + 1, end + 1, end + 2))
+    groups.append(((23,), end + 2, end + 2, end + 2))
+    weave = {}
+    quant = {}
+    weave.setdefault(HEAD[0], []).append(("V", 0, 0, 0, 512))
+    quant.setdefault(HEAD[1], []).append((0, 0))
+    weave.setdefault(HEAD[2], []).append(("V", 0, 1, 0, 512))
+    quant.setdefault(HEAD[3], []).append((0, 1))
+    for c in (1, 2):
+        for g in range(PASSES):
+            for h in range(2):
+                weave.setdefault(U_FIRST[c - 1] + 2 * g + h, []).append((U_ENG[2 * g + h], c, g, 256 * h, 256 * h + 256))
+            quant.setdefault(U_FIRST[c - 1] + 2 * g + 2, []).append((c, g))
+    ops = [("RA", 0), ("ca", 0)]
+    for n in range(end + 4):
+        for tiles, ts, tcs, qs in groups:
+            if ts == n:
+                ops.append(("tr", tiles))
+        ms = [m for m in range(TILES) if ru_step[m] == n]
+        for m in ms:
+            ops.append(("RU", m))
+        if n + 1 < TILES:
+            ops.append(("RA", n + 1))
+        if n < TILES:
+            ops.append(("RB", n))
+        if n + 1 < TILES:
+            ops.append(("ca", n + 1))
+        vs = [("y", m) for m in ms]
+        if 0 <= n - 1 < TILES:
+            vs = vs[:1] + [("p", n - 1)] + vs[1:]
+        for v in vs:
+            ops.append(v)
+            if v[0] == "y":
+                ops.append(("sty", v[1]))
+                if POOL_CASTS and v[1] < TILES - 1:
+                    ops.append(("castG", v[1]))
+        for m in range(TILES):
+            if m == TILES - 1:
+                if ru_step[m] == n:
+                    ops.append(("castV", m))
+            elif not POOL_CASTS and ru_step[m] + 1 == n:
+                ops.append(("castV", m))
+        if 0 <= n - RS_LAG < TILES:
+            ops.append(("rs", n - RS_LAG))
+        for tiles, ts, tcs, qs in groups:
+            if tcs == n:
+                ops.append(("tc", tiles))
+        for piece in weave.get(n, []):
+            ops.append(("ui", piece))
+        for q in quant.get(n, []):
+            ops.append(("qu", q))
+        for tiles, ts, tcs, qs in groups:
+            if qs == n:
+                if tiles[0] < 20:
+                    tiles = tuple(range(tiles[0], tiles[0] + 4))
+                ops.append(("qy", tiles))
+                ops.append(("stw", tiles))
+    return ops
+
+
+def tile_replicate_call_eqtl_t_k3_kernel(tc, x_words, x_scales, a_words, a_scales, b_words, b_scales, u, out_0, out_1, out_2):
+    nc = tc.nc
+    with ExitStack() as ctx:
+        keep = ctx.enter_context(tc.tile_pool(name="keep", bufs=1))
+        flow = ctx.enter_context(tc.tile_pool(name="flow", bufs=4))
+        psum = ctx.enter_context(tc.psum_pool(name="psum", bufs=2))
+        ctx.enter_context(tc.manual_schedule())
+
+        xw = keep.tile([P, PASSES, G], U32, align_bytes=64)
+        aw = keep.tile([P, PASSES, 2 * V], U8, align_bytes=64)
+        bw = keep.tile([P, PASSES, V], U32, align_bytes=64)
+        xs = keep.tile([P, PASSES, G], U8, align_bytes=64)
+        as_ = keep.tile([P, PASSES, V], U8, align_bytes=64)
+        bs = keep.tile([P, PASSES, V], U8, align_bytes=64)
+        uraw = keep.tile([P, CHUNKS, PASSES, PACK, CHUNK], BF16, align_bytes=64)
+        uweave = keep.tile([P, CHUNKS, PASSES, CHUNK, PACK], BF16, align_bytes=64)
+        uw = keep.tile([P, CHUNKS, PASSES, CHUNK], U32, align_bytes=64)
+        us = keep.tile([P, CHUNKS, PASSES, CHUNK], U8, align_bytes=64)
+        yw = keep.tile([P, CHUNKS, G], U32, align_bytes=64)
+        ys = keep.tile([P, CHUNKS, G], U8, align_bytes=64)
+        yt = keep.tile([P, CHUNKS, G, PACK], BF16, align_bytes=64)
+        ident = keep.tile([P, P], F32, align_bytes=64)
+        first = keep.tile([P, 8], F32, align_bytes=64)
+
+        x_src = x_words.rearrange("g p n t -> p g (n t)").bitcast(I32)
+        a_src = a_words.rearrange("g p n -> p g n").bitcast(I32)
+        b_src = b_words.rearrange("g p n t -> p g (n t)").bitcast(I32)
+        xs_src = x_scales.rearrange("g q n -> q g n").bitcast(I32)
+        as_src = a_scales.rearrange("g q n -> q g n").bitcast(I32)
+        bs_src = b_scales.rearrange("g q n -> q g n").bitcast(I32)
+        u_src = u.rearrange("(g p j) v -> g p j v", p=P, j=PACK)
+        w_dst = out_1.rearrange("c p m t -> c p (m t)").bitcast(I32)
+        s_dst = out_2.bitcast(I32)
+
+        def load_x(lo, hi):
+            nc.sync.dma_start(out=xw[:, :, lo:hi].bitcast(I32), in_=x_src[:, :, lo:hi])
+
+        def load_a(c):
+            nc.sync.dma_start(out=aw[:].bitcast(I32)[:, :, 256 * c : 256 * (c + 1)], in_=a_src[:, :, 256 * c : 256 * (c + 1)])
+
+        def load_b(c):
+            cols = slice(CHUNK * c, CHUNK * (c + 1))
+            nc.sync.dma_start(out=bw[:, :, cols].bitcast(I32), in_=b_src[:, :, cols])
+
+        def load_u(c, g):
+            nc.sync.dma_start(out=uraw[:, c, g], in_=u_src[g, :, :, CHUNK * c : CHUNK * (c + 1)])
+
+        nc.vector.memset(first[:], 1.0)
+        nc.vector.memset(xs[:].bitcast(I32), 0)
+        nc.vector.memset(as_[:].bitcast(I32), 0)
+        nc.vector.memset(bs[:].bitcast(I32), 0)
+        nc.scalar.activation(out=first[:, 4:8], in_=first[:, 0:4], func=ACT.Abs_reciprocal_sqrt)
+
+        load_x(0, 256)
+        load_a(0)
+        for q in range(4):
+            nc.sync.dma_start(out=xs[32 * q : 32 * q + 4].bitcast(I32), in_=xs_src[4 * q : 4 * q + 4])
+        for q in range(4):
+            eng = nc.sync if q < 2 else nc.gpsimd
+            eng.dma_start(out=as_[32 * q : 32 * q + 4].bitcast(I32), in_=as_src[4 * q : 4 * q + 4])
+        load_b(0)
+        for q in range(4):
+            nc.sync.dma_start(out=bs[32 * q + 4 : 32 * q + 8].bitcast(I32), in_=bs_src[4 * q : 4 * q + 4])
+        load_x(256, 512)
+        load_x(512, 1024)
+        load_u(0, 0)
+        load_u(0, 1)
+        for c in (1, 2):
+            load_a(c)
+            load_b(c)
+            load_u(c, 0)
+            load_u(c, 1)
+        make_identity(nc, ident[:])
+
+        if WARM:
+            warm = keep.tile([P, CHUNK], BF16, align_bytes=64)
+            nc.vector.memset(warm[:], 0.0)
+            junk = psum.tile([P, CHUNK], F32, tag="turn")
+            for w in range(WARM):
+                nc.tensor.matmul(out=junk[:], lhsT=warm[:, 0:P], rhs=warm[:], start=True, stop=True)
+
+        held = {}
+
+        def product(tag, n, rhs, rhs_scale):
+            genes = slice(P * (n % GENE_TILES), P * (n % GENE_TILES + 1))
+            acc = psum.tile([P, CHUNK], F32, tag=tag, name=tag)
+            held[tag, n] = acc
+            for g in range(PASSES):
+                nc.tensor.matmul_mx(out=acc[:], lhsT=xw[:, g, genes].bitcast(FP8X4), lhsT_scale=xs[:, g, genes],
+                                    rhs=rhs(g), rhs_scale=rhs_scale(g), start=(g == 0), stop=(g == PASSES - 1))
+
+        def cols_of(n):
+            c = n // GENE_TILES
+            return slice(CHUNK * c, CHUNK * (c + 1))
+
+        def ra(n):
+            c = n // GENE_TILES
+            product("ra", n, lambda g: aw[:, g, 2 * CHUNK * c : 2 * CHUNK * (c + 1)].bitcast(FP4X4), lambda g: as_[:, g, cols_of(n)])
+
+        def rb(n):
+            product("rb", n, lambda g: bw[:, g, cols_of(n)].bitcast(FP8X4), lambda g: bs[4:, g, cols_of(n)])
+
+        def ru(n):
+            c = n // GENE_TILES
+            product("ru", n, lambda g: uw[:, c, g].bitcast(FP8X4), lambda g: us[:, c, g])
+
+        def copy_ra(n):
+            t = flow.tile([P, CHUNK], F32, tag="ra_sb", name="ra_sb", bufs=4)
+            held["ra_sb", n] = t
+            nc.scalar.copy(out=t[:], in_=held["ra", n][:])
+
+        def explained(n):
+            t = flow.tile([P, CHUNK], F32, tag="prod", name="prod", bufs=4)
+            held["prod", n] = t
+            nc.vector.tensor_tensor(out=t[:], in0=held["rb", n][:], in1=held["ra_sb", n][:], op=ALU.mult)
+
+        def root(n):
+            t = flow.tile([P, CHUNK], F32, tag="root", name="root", bufs=FIRST_LAG + 3)
+            held["root", n] = t
+            nc.scalar.activation(out=t[:], in_=held["prod", n][:], func=ACT.Abs_reciprocal_sqrt, scale=-1.0, bias=1.0)
+
+        def result(n):
+            t = flow.tile([P, CHUNK], F32, tag="y", name="y", bufs=8)
+            held["y", n] = t
+            nc.vector.tensor_tensor(out=t[:], in0=held["ru", n][:], in1=held["root", n][:], op=ALU.mult)
+
+        def store_y(n):
+            i = n % GENE_TILES
+            nc.sync.dma_start(out=out_0[P * i : P * (i + 1), cols_of(n)], in_=held["y", n][:])
+
+        def cast(n, on_pool):
+            t = flow.tile([P, 2, P, 2], BF16, tag="ybf", name="ybf", bufs=8, align_bytes=64)
+            held["ybf", n] = t
+            src = held["y", n][:].rearrange("g (p h e) -> g h p e", h=2, e=2)
+            if on_pool:
+                nc.gpsimd.tensor_scalar(out=t[:], in0=src, scalar1=1.0, scalar2=-0.0, op0=ALU.mult, op1=ALU.add)
+            else:
+                nc.vector.tensor_copy(out=t[:], in_=src)
+
+        def turn(tiles):
+            bank = psum.tile([P, 2, 2, P], F32, tag="turn", name="turn")
+            held["turn", tiles] = bank
+            for a, n in enumerate(tiles):
+                words = held["ybf", n][:].rearrange("g h p e -> g h (p e)").bitcast(F32)
+                for h in range(2):
+                    nc.tensor.transpose(out=bank[:, a, h, :], in_=words[:, h, :], identity=ident[:])
+
+        def genes_of(tiles):
+            lo = P * (tiles[0] % GENE_TILES)
+            return slice(lo, lo + P * len(tiles))
+
+        def copy_turned(tiles):
+            c = tiles[0] // GENE_TILES
+            dst = yt[:, c, genes_of(tiles), :].bitcast(F32).rearrange("p (a g) h -> p a g h", g=P)
+            nc.scalar.copy(out=dst, in_=held["turn", tiles][:, 0 : len(tiles)].rearrange("p a h g -> p a g h"))
+
+        def weave_u(piece):
+            eng, c, g, lo, hi = piece
+            dst = uweave[:, c, g, lo:hi, :]
+            src = uraw[:, c, g, :, lo:hi].rearrange("p j w -> p w j")
+            if eng == "V":
+                nc.vector.tensor_copy(out=dst, in_=src)
+            else:
+                nc.scalar.copy(out=dst, in_=src)
+
+        def quant_u(cg):
+            c, g = cg
+            nc.vector.quantize_mx(out=uw[:, c, g].bitcast(FP8X4), scales=us[:, c, g], in_=uweave[:, c, g].rearrange("p w j -> p (w j)"))
+
+        def quant_y(tiles):
+            c = tiles[0] // GENE_TILES
+            genes = genes_of(tiles)
+            nc.vector.quantize_mx(out=yw[:, c, genes].bitcast(FP8X4), scales=ys[:, c, genes], in_=yt[:, c, genes, :].rearrange("p g t -> p (g t)"))
+
+        def store_planes(tiles):
+            c = tiles[0] // GENE_TILES
+            genes = genes_of(tiles)
+            nc.sync.dma_start(out=w_dst[c, :, genes], in_=yw[:, c, genes].bitcast(I32))
+            if tiles[-1] % GENE_TILES == GENE_TILES - 1:
+                for q in range(4):
+                    nc.sync.dma_start(out=s_dst[c, 4 * q : 4 * q + 4, :], in_=ys[32 * q : 32 * q + 4, c, :].bitcast(I32))
+
+        steps = {"RA": ra, "RB": rb, "RU": ru, "ca": copy_ra, "p": explained, "rs": root, "y": result, "sty": store_y,
+                 "castG": lambda n: cast(n, True), "castV": lambda n: cast(n, False), "tr": turn, "tc": copy_turned,
+                 "ui": weave_u, "qu": quant_u, "qy": quant_y, "stw": store_planes}
+        for name, arg in program_order():
+            steps[name](arg)

@@ -25,16 +25,22 @@ CHUNKS = V // CHUNK
 GENE_TILES = G // P
 TILES = CHUNKS * GENE_TILES
 
-FIRST_LAG = 9
-DOUBLE_STEPS = (10, 13, 16, 19, 22)
-POOL_CASTS = True
+FIRST_LAG = 10
+DOUBLE_STEPS = (10, 12, 14, 16, 18, 20, 22)
+POOL_CASTS = False
 RS_LAG = 2
-TR_LAG = 3
+TR_LAG = 4
 TC_LAG = 0
-QY_LAG = 2
-HEAD = (4, 6, 6, 8)
-U_FIRST = (9, 15)
-U_ENG = "SSSV"
+QY_LAG = 1
+HEAD = (3, 8, 5, 7)
+U_FIRST = (8, 14)
+U_ENG = "SVSS"
+X_PIECES = ((0, 256), (256, 512), (512, 1024))
+LOADS = (("x", 0), ("a", 0), ("xs", 0), ("as", 0), ("b", 0), ("bs", 0), ("x", 1), ("x", 2), ("u", 0), ("u", 1), ("a", 1), ("b", 1), ("u", 2), ("u", 3), ("a", 2), ("b", 2), ("u", 4), ("u", 5))
+HEAD_SPLIT = 512
+RS_HEAD = 0
+TAIL = (((20, 21), 1, 1, 1), ((22,), 1, 1, 2), ((23,), 2, 2, 2))
+LEAD = 1
 WARM = 0
 
 
@@ -52,21 +58,26 @@ def program_order():
         ts = ru_step[4 * j + 3] + TR_LAG
         groups.append(((4 * j, 4 * j + 1), ts, ts + TC_LAG, ts + QY_LAG))
         groups.append(((4 * j + 2, 4 * j + 3), ts, ts + TC_LAG, None))
-    groups.append(((20, 21), end + 1, end + 1, end + 2))
-    groups.append(((22,), end + 1, end + 1, end + 2))
-    groups.append(((23,), end + 2, end + 2, end + 2))
+    for tiles, ts, tcs, qs in TAIL:
+        groups.append((tiles, end + ts, end + tcs, end + qs))
     weave = {}
     quant = {}
-    weave.setdefault(HEAD[0], []).append(("V", 0, 0, 0, 512))
+    weave.setdefault(HEAD[0], []).append(("V", 0, 0, 0, HEAD_SPLIT))
+    if HEAD_SPLIT < 512:
+        weave[HEAD[0]].append(("S", 0, 0, HEAD_SPLIT, 512))
     quant.setdefault(HEAD[1], []).append((0, 0))
-    weave.setdefault(HEAD[2], []).append(("V", 0, 1, 0, 512))
+    weave.setdefault(HEAD[2], []).append(("V", 0, 1, 0, HEAD_SPLIT))
+    if HEAD_SPLIT < 512:
+        weave[HEAD[2]].append(("S", 0, 1, HEAD_SPLIT, 512))
     quant.setdefault(HEAD[3], []).append((0, 1))
     for c in (1, 2):
         for g in range(PASSES):
             for h in range(2):
                 weave.setdefault(U_FIRST[c - 1] + 2 * g + h, []).append((U_ENG[2 * g + h], c, g, 256 * h, 256 * h + 256))
             quant.setdefault(U_FIRST[c - 1] + 2 * g + 2, []).append((c, g))
-    ops = [("RA", 0), ("ca", 0)]
+    ops = []
+    for n in range(LEAD):
+        ops += [("RA", n), ("ca", n)]
     for n in range(end + 4):
         for tiles, ts, tcs, qs in groups:
             if ts == n:
@@ -74,29 +85,29 @@ def program_order():
         ms = [m for m in range(TILES) if ru_step[m] == n]
         for m in ms:
             ops.append(("RU", m))
-        if n + 1 < TILES:
-            ops.append(("RA", n + 1))
+        if n + LEAD < TILES:
+            ops.append(("RA", n + LEAD))
         if n < TILES:
             ops.append(("RB", n))
-        if n + 1 < TILES:
-            ops.append(("ca", n + 1))
+        if n + LEAD < TILES:
+            ops.append(("ca", n + LEAD))
         vs = [("y", m) for m in ms]
         if 0 <= n - 1 < TILES:
             vs = vs[:1] + [("p", n - 1)] + vs[1:]
         for v in vs:
+            if v == ("y", TILES - 1):
+                ops.append(("yb", TILES - 1))
             ops.append(v)
             if v[0] == "y":
                 ops.append(("sty", v[1]))
                 if POOL_CASTS and v[1] < TILES - 1:
                     ops.append(("castG", v[1]))
         for m in range(TILES):
-            if m == TILES - 1:
-                if ru_step[m] == n:
-                    ops.append(("castV", m))
-            elif not POOL_CASTS and ru_step[m] + 1 == n:
+            if m < TILES - 1 and not POOL_CASTS and ru_step[m] + 1 == n:
                 ops.append(("castV", m))
-        if 0 <= n - RS_LAG < TILES:
-            ops.append(("rs", n - RS_LAG))
+        for k in range(TILES):
+            if max(k + RS_LAG, RS_HEAD + k // 2) == n:
+                ops.append(("rs", k))
         for tiles, ts, tcs, qs in groups:
             if tcs == n:
                 ops.append(("tc", tiles))
@@ -121,9 +132,9 @@ def tile_replicate_call_eqtl_t_k3_kernel(tc, x_words, x_scales, a_words, a_scale
         psum = ctx.enter_context(tc.psum_pool(name="psum", bufs=2))
         ctx.enter_context(tc.manual_schedule())
 
-        xw = keep.tile([P, PASSES, G], U32, align_bytes=64)
-        aw = keep.tile([P, PASSES, 2 * V], U8, align_bytes=64)
-        bw = keep.tile([P, PASSES, V], U32, align_bytes=64)
+        xw = [keep.tile([P, PASSES, hi - lo], U32, align_bytes=64, name="xw%d" % lo) for lo, hi in X_PIECES]
+        aw = [keep.tile([P, PASSES, 2 * CHUNK], U8, align_bytes=64, name="aw%d" % c) for c in range(CHUNKS)]
+        bw = [keep.tile([P, PASSES, CHUNK], U32, align_bytes=64, name="bw%d" % c) for c in range(CHUNKS)]
         xs = keep.tile([P, PASSES, G], U8, align_bytes=64)
         as_ = keep.tile([P, PASSES, V], U8, align_bytes=64)
         bs = keep.tile([P, PASSES, V], U8, align_bytes=64)
@@ -147,44 +158,45 @@ def tile_replicate_call_eqtl_t_k3_kernel(tc, x_words, x_scales, a_words, a_scale
         w_dst = out_1.rearrange("c p m t -> c p (m t)").bitcast(I32)
         s_dst = out_2.bitcast(I32)
 
-        def load_x(lo, hi):
-            nc.sync.dma_start(out=xw[:, :, lo:hi].bitcast(I32), in_=x_src[:, :, lo:hi])
+        def load_x(k, eng=nc.sync):
+            lo, hi = X_PIECES[k]
+            eng.dma_start(out=xw[k][:].bitcast(I32), in_=x_src[:, :, lo:hi])
 
-        def load_a(c):
-            nc.sync.dma_start(out=aw[:].bitcast(I32)[:, :, 256 * c : 256 * (c + 1)], in_=a_src[:, :, 256 * c : 256 * (c + 1)])
+        def load_a(c, eng=nc.sync):
+            eng.dma_start(out=aw[c][:].bitcast(I32), in_=a_src[:, :, 256 * c : 256 * (c + 1)])
 
-        def load_b(c):
+        def load_b(c, eng=nc.sync):
             cols = slice(CHUNK * c, CHUNK * (c + 1))
-            nc.sync.dma_start(out=bw[:, :, cols].bitcast(I32), in_=b_src[:, :, cols])
+            eng.dma_start(out=bw[c][:].bitcast(I32), in_=b_src[:, :, cols])
 
         def load_u(c, g):
             nc.sync.dma_start(out=uraw[:, c, g], in_=u_src[g, :, :, CHUNK * c : CHUNK * (c + 1)])
 
         nc.vector.memset(first[:], 1.0)
-        nc.vector.memset(xs[:].bitcast(I32), 0)
+        nc.gpsimd.memset(xs[:].bitcast(I32), 0)
         nc.vector.memset(as_[:].bitcast(I32), 0)
         nc.vector.memset(bs[:].bitcast(I32), 0)
         nc.scalar.activation(out=first[:, 4:8], in_=first[:, 0:4], func=ACT.Abs_reciprocal_sqrt)
 
-        load_x(0, 256)
-        load_a(0)
-        for q in range(4):
-            nc.sync.dma_start(out=xs[32 * q : 32 * q + 4].bitcast(I32), in_=xs_src[4 * q : 4 * q + 4])
-        for q in range(4):
-            eng = nc.sync if q < 2 else nc.gpsimd
-            eng.dma_start(out=as_[32 * q : 32 * q + 4].bitcast(I32), in_=as_src[4 * q : 4 * q + 4])
-        load_b(0)
-        for q in range(4):
-            nc.sync.dma_start(out=bs[32 * q + 4 : 32 * q + 8].bitcast(I32), in_=bs_src[4 * q : 4 * q + 4])
-        load_x(256, 512)
-        load_x(512, 1024)
-        load_u(0, 0)
-        load_u(0, 1)
-        for c in (1, 2):
-            load_a(c)
-            load_b(c)
-            load_u(c, 0)
-            load_u(c, 1)
+        def load_scales(plane, src, row):
+            for q in range(4):
+                nc.sync.dma_start(out=plane[32 * q + row : 32 * q + row + 4].bitcast(I32), in_=src[4 * q : 4 * q + 4])
+
+        for kind, k in LOADS:
+            if kind == "x":
+                load_x(k)
+            elif kind == "a":
+                load_a(k)
+            elif kind == "b":
+                load_b(k)
+            elif kind == "u":
+                load_u(k // 2, k % 2)
+            elif kind == "xs":
+                load_scales(xs, xs_src, 0)
+            elif kind == "as":
+                load_scales(as_, as_src, 0)
+            else:
+                load_scales(bs, bs_src, 4)
         make_identity(nc, ident[:])
 
         if WARM:
@@ -198,10 +210,12 @@ def tile_replicate_call_eqtl_t_k3_kernel(tc, x_words, x_scales, a_words, a_scale
 
         def product(tag, n, rhs, rhs_scale):
             genes = slice(P * (n % GENE_TILES), P * (n % GENE_TILES + 1))
+            k = [genes.start < hi for lo, hi in X_PIECES].index(True)
+            local = slice(genes.start - X_PIECES[k][0], genes.stop - X_PIECES[k][0])
             acc = psum.tile([P, CHUNK], F32, tag=tag, name=tag)
             held[tag, n] = acc
             for g in range(PASSES):
-                nc.tensor.matmul_mx(out=acc[:], lhsT=xw[:, g, genes].bitcast(FP8X4), lhsT_scale=xs[:, g, genes],
+                nc.tensor.matmul_mx(out=acc[:], lhsT=xw[k][:, g, local].bitcast(FP8X4), lhsT_scale=xs[:, g, genes],
                                     rhs=rhs(g), rhs_scale=rhs_scale(g), start=(g == 0), stop=(g == PASSES - 1))
 
         def cols_of(n):
@@ -210,27 +224,27 @@ def tile_replicate_call_eqtl_t_k3_kernel(tc, x_words, x_scales, a_words, a_scale
 
         def ra(n):
             c = n // GENE_TILES
-            product("ra", n, lambda g: aw[:, g, 2 * CHUNK * c : 2 * CHUNK * (c + 1)].bitcast(FP4X4), lambda g: as_[:, g, cols_of(n)])
+            product("ra", n, lambda g: aw[c][:, g, :].bitcast(FP4X4), lambda g: as_[:, g, cols_of(n)])
 
         def rb(n):
-            product("rb", n, lambda g: bw[:, g, cols_of(n)].bitcast(FP8X4), lambda g: bs[4:, g, cols_of(n)])
+            product("rb", n, lambda g: bw[n // GENE_TILES][:, g, :].bitcast(FP8X4), lambda g: bs[4:, g, cols_of(n)])
 
         def ru(n):
             c = n // GENE_TILES
             product("ru", n, lambda g: uw[:, c, g].bitcast(FP8X4), lambda g: us[:, c, g])
 
         def copy_ra(n):
-            t = flow.tile([P, CHUNK], F32, tag="ra_sb", name="ra_sb", bufs=4)
+            t = flow.tile([P, CHUNK], F32, tag="ra_sb", name="ra_sb", bufs=LEAD + 3)
             held["ra_sb", n] = t
             nc.scalar.copy(out=t[:], in_=held["ra", n][:])
 
         def explained(n):
-            t = flow.tile([P, CHUNK], F32, tag="prod", name="prod", bufs=4)
+            t = flow.tile([P, CHUNK], F32, tag="prod", name="prod", bufs=8)
             held["prod", n] = t
             nc.vector.tensor_tensor(out=t[:], in0=held["rb", n][:], in1=held["ra_sb", n][:], op=ALU.mult)
 
         def root(n):
-            t = flow.tile([P, CHUNK], F32, tag="root", name="root", bufs=FIRST_LAG + 3)
+            t = flow.tile([P, CHUNK], F32, tag="root", name="root", bufs=FIRST_LAG + 1)
             held["root", n] = t
             nc.scalar.activation(out=t[:], in_=held["prod", n][:], func=ACT.Abs_reciprocal_sqrt, scale=-1.0, bias=1.0)
 
@@ -244,13 +258,20 @@ def tile_replicate_call_eqtl_t_k3_kernel(tc, x_words, x_scales, a_words, a_scale
             nc.sync.dma_start(out=out_0[P * i : P * (i + 1), cols_of(n)], in_=held["y", n][:])
 
         def cast(n, on_pool):
-            t = flow.tile([P, 2, P, 2], BF16, tag="ybf", name="ybf", bufs=8, align_bytes=64)
+            t = flow.tile([P, 2, P, 2], BF16, tag="ybf", name="ybf", bufs=12, align_bytes=64)
             held["ybf", n] = t
             src = held["y", n][:].rearrange("g (p h e) -> g h p e", h=2, e=2)
             if on_pool:
                 nc.gpsimd.tensor_scalar(out=t[:], in0=src, scalar1=1.0, scalar2=-0.0, op0=ALU.mult, op1=ALU.add)
             else:
                 nc.vector.tensor_copy(out=t[:], in_=src)
+
+        def result_bf16(n):
+            t = flow.tile([P, 2, P, 2], BF16, tag="ybf", name="ybf", bufs=12, align_bytes=64)
+            held["ybf", n] = t
+            order = "g (p h e) -> g h p e"
+            nc.vector.tensor_tensor(out=t[:], in0=held["ru", n][:].rearrange(order, h=2, e=2),
+                                    in1=held["root", n][:].rearrange(order, h=2, e=2), op=ALU.mult)
 
         def turn(tiles):
             bank = psum.tile([P, 2, 2, P], F32, tag="turn", name="turn")
@@ -271,8 +292,8 @@ def tile_replicate_call_eqtl_t_k3_kernel(tc, x_words, x_scales, a_words, a_scale
 
         def weave_u(piece):
             eng, c, g, lo, hi = piece
-            dst = uweave[:, c, g, lo:hi, :]
-            src = uraw[:, c, g, :, lo:hi].rearrange("p j w -> p w j")
+            dst = uweave[:, c, g, lo:hi, :].rearrange("p (w i) j -> p w j i", i=4)
+            src = uraw[:, c, g, :, lo:hi].rearrange("p j (w i) -> p w j i", i=4)
             if eng == "V":
                 nc.vector.tensor_copy(out=dst, in_=src)
             else:
@@ -293,10 +314,10 @@ def tile_replicate_call_eqtl_t_k3_kernel(tc, x_words, x_scales, a_words, a_scale
             nc.sync.dma_start(out=w_dst[c, :, genes], in_=yw[:, c, genes].bitcast(I32))
             if tiles[-1] % GENE_TILES == GENE_TILES - 1:
                 for q in range(4):
-                    nc.sync.dma_start(out=s_dst[c, 4 * q : 4 * q + 4, :], in_=ys[32 * q : 32 * q + 4, c, :].bitcast(I32))
+                    (nc.scalar if c == CHUNKS - 1 and q % 2 == 0 else nc.sync).dma_start(out=s_dst[c, 4 * q : 4 * q + 4, :], in_=ys[32 * q : 32 * q + 4, c, :].bitcast(I32))
 
         steps = {"RA": ra, "RB": rb, "RU": ru, "ca": copy_ra, "p": explained, "rs": root, "y": result, "sty": store_y,
-                 "castG": lambda n: cast(n, True), "castV": lambda n: cast(n, False), "tr": turn, "tc": copy_turned,
+                 "castG": lambda n: cast(n, True), "castV": lambda n: cast(n, False), "tr": turn, "yb": result_bf16, "tc": copy_turned,
                  "ui": weave_u, "qu": quant_u, "qy": quant_y, "stw": store_planes}
         for name, arg in program_order():
             steps[name](arg)

@@ -25,23 +25,27 @@ CHUNKS = V // CHUNK
 GENE_TILES = G // P
 TILES = CHUNKS * GENE_TILES
 
-FIRST_LAG = 10
-DOUBLE_STEPS = (10, 12, 14, 16, 18, 20, 22)
-POOL_CASTS = False
+FIRST_LAG = 7
+DOUBLE_STEPS = (7, 8, 13, 20)
+POOL_TILES = ()
+CAST_LAG = 1
+P_FIRST = 0
 RS_LAG = 2
 TR_LAG = 4
 TC_LAG = 0
 QY_LAG = 1
-HEAD = (3, 8, 5, 7)
-U_FIRST = (8, 14)
+HEAD = (1, 2, 3, 5)
+U_FIRST = (5, 11)
 U_ENG = "SVSS"
 X_PIECES = ((0, 256), (256, 512), (512, 1024))
-LOADS = (("x", 0), ("a", 0), ("xs", 0), ("as", 0), ("b", 0), ("bs", 0), ("x", 1), ("x", 2), ("u", 0), ("u", 1), ("a", 1), ("b", 1), ("u", 2), ("u", 3), ("a", 2), ("b", 2), ("u", 4), ("u", 5))
-HEAD_SPLIT = 512
+LOADS = (("x", 0), ("xs", 0), ("a", 0), ("as", 0), ("b", 0), ("bs", 0), ("as", 1), ("bs", 1), ("x", 1), ("u", 0), ("x", 2), ("u", 1), ("a", 1), ("b", 1), ("u", 2), ("u", 3), ("u", 4), ("a", 2), ("b", 2), ("u", 5))
+HEAD_SPLIT = 384
 RS_HEAD = 0
-TAIL = (((20, 21), 1, 1, 1), ((22,), 1, 1, 2), ((23,), 2, 2, 2))
+TAIL = (((20, 21), 1, 1, 2), ((22,), 1, 1, 2), ((23,), 2, 2, 2))
 LEAD = 1
-WARM = 0
+S_PIECES = ((0, CHUNK), (CHUNK, V))
+POOL_LOADS = (("bs", 0), ("as", 1), ("bs", 1))
+WARM = 7
 
 
 def program_order():
@@ -93,17 +97,17 @@ def program_order():
             ops.append(("ca", n + LEAD))
         vs = [("y", m) for m in ms]
         if 0 <= n - 1 < TILES:
-            vs = vs[:1] + [("p", n - 1)] + vs[1:]
+            vs = vs[:P_FIRST] + [("p", n - 1)] + vs[P_FIRST:]
         for v in vs:
             if v == ("y", TILES - 1):
                 ops.append(("yb", TILES - 1))
             ops.append(v)
             if v[0] == "y":
                 ops.append(("sty", v[1]))
-                if POOL_CASTS and v[1] < TILES - 1:
+                if v[1] in POOL_TILES:
                     ops.append(("castG", v[1]))
         for m in range(TILES):
-            if m < TILES - 1 and not POOL_CASTS and ru_step[m] + 1 == n:
+            if m < TILES - 1 and m not in POOL_TILES and ru_step[m] + CAST_LAG == n:
                 ops.append(("castV", m))
         for k in range(TILES):
             if max(k + RS_LAG, RS_HEAD + k // 2) == n:
@@ -136,8 +140,8 @@ def tile_replicate_call_eqtl_t_k3_kernel(tc, x_words, x_scales, a_words, a_scale
         aw = [keep.tile([P, PASSES, 2 * CHUNK], U8, align_bytes=64, name="aw%d" % c) for c in range(CHUNKS)]
         bw = [keep.tile([P, PASSES, CHUNK], U32, align_bytes=64, name="bw%d" % c) for c in range(CHUNKS)]
         xs = keep.tile([P, PASSES, G], U8, align_bytes=64)
-        as_ = keep.tile([P, PASSES, V], U8, align_bytes=64)
-        bs = keep.tile([P, PASSES, V], U8, align_bytes=64)
+        as_ = [keep.tile([P, PASSES, hi - lo], U8, align_bytes=64, name="as%d" % lo) for lo, hi in S_PIECES]
+        bs = [keep.tile([P, PASSES, hi - lo], U8, align_bytes=64, name="bs%d" % lo) for lo, hi in S_PIECES]
         uraw = keep.tile([P, CHUNKS, PASSES, PACK, CHUNK], BF16, align_bytes=64)
         uweave = keep.tile([P, CHUNKS, PASSES, CHUNK, PACK], BF16, align_bytes=64)
         uw = keep.tile([P, CHUNKS, PASSES, CHUNK], U32, align_bytes=64)
@@ -174,13 +178,18 @@ def tile_replicate_call_eqtl_t_k3_kernel(tc, x_words, x_scales, a_words, a_scale
 
         nc.vector.memset(first[:], 1.0)
         nc.gpsimd.memset(xs[:].bitcast(I32), 0)
-        nc.vector.memset(as_[:].bitcast(I32), 0)
-        nc.vector.memset(bs[:].bitcast(I32), 0)
+        nc.vector.memset(as_[0][:].bitcast(I32), 0)
+        nc.vector.memset(bs[0][:].bitcast(I32), 0)
+        if WARM:
+            warm = keep.tile([P, CHUNK], BF16, align_bytes=64)
+            nc.vector.memset(warm[:], 0.0)
+        nc.vector.memset(as_[1][:].bitcast(I32), 0)
+        nc.vector.memset(bs[1][:].bitcast(I32), 0)
         nc.scalar.activation(out=first[:, 4:8], in_=first[:, 0:4], func=ACT.Abs_reciprocal_sqrt)
 
-        def load_scales(plane, src, row):
+        def load_scales(plane, src, row, eng=nc.sync):
             for q in range(4):
-                nc.sync.dma_start(out=plane[32 * q + row : 32 * q + row + 4].bitcast(I32), in_=src[4 * q : 4 * q + 4])
+                eng.dma_start(out=plane[32 * q + row : 32 * q + row + 4].bitcast(I32), in_=src[4 * q : 4 * q + 4])
 
         for kind, k in LOADS:
             if kind == "x":
@@ -194,14 +203,12 @@ def tile_replicate_call_eqtl_t_k3_kernel(tc, x_words, x_scales, a_words, a_scale
             elif kind == "xs":
                 load_scales(xs, xs_src, 0)
             elif kind == "as":
-                load_scales(as_, as_src, 0)
+                load_scales(as_[k], as_src[:, :, S_PIECES[k][0] // 4 : S_PIECES[k][1] // 4], 0, nc.gpsimd if (kind, k) in POOL_LOADS else nc.sync)
             else:
-                load_scales(bs, bs_src, 4)
+                load_scales(bs[k], bs_src[:, :, S_PIECES[k][0] // 4 : S_PIECES[k][1] // 4], 4, nc.gpsimd if (kind, k) in POOL_LOADS else nc.sync)
         make_identity(nc, ident[:])
 
         if WARM:
-            warm = keep.tile([P, CHUNK], BF16, align_bytes=64)
-            nc.vector.memset(warm[:], 0.0)
             junk = psum.tile([P, CHUNK], F32, tag="turn")
             for w in range(WARM):
                 nc.tensor.matmul(out=junk[:], lhsT=warm[:, 0:P], rhs=warm[:], start=True, stop=True)
@@ -222,12 +229,18 @@ def tile_replicate_call_eqtl_t_k3_kernel(tc, x_words, x_scales, a_words, a_scale
             c = n // GENE_TILES
             return slice(CHUNK * c, CHUNK * (c + 1))
 
+        def plane_of(planes, row, g, n):
+            c = n // GENE_TILES
+            k = min(c, 1)
+            lo = CHUNK * c - S_PIECES[k][0]
+            return planes[k][row:, g, lo : lo + CHUNK]
+
         def ra(n):
             c = n // GENE_TILES
-            product("ra", n, lambda g: aw[c][:, g, :].bitcast(FP4X4), lambda g: as_[:, g, cols_of(n)])
+            product("ra", n, lambda g: aw[c][:, g, :].bitcast(FP4X4), lambda g: plane_of(as_, 0, g, n))
 
         def rb(n):
-            product("rb", n, lambda g: bw[n // GENE_TILES][:, g, :].bitcast(FP8X4), lambda g: bs[4:, g, cols_of(n)])
+            product("rb", n, lambda g: bw[n // GENE_TILES][:, g, :].bitcast(FP8X4), lambda g: plane_of(bs, 4, g, n))
 
         def ru(n):
             c = n // GENE_TILES

@@ -26,25 +26,29 @@ GENE_TILES = G // P
 TILES = CHUNKS * GENE_TILES
 
 FIRST_LAG = 7
-DOUBLE_STEPS = (7, 8, 13, 20)
+DOUBLE_STEPS = (14, 22)
 POOL_TILES = ()
 CAST_LAG = 1
 P_FIRST = 0
 RS_LAG = 2
-TR_LAG = 4
+TR_LAG = 3
 TC_LAG = 0
-QY_LAG = 1
-HEAD = (1, 2, 3, 5)
-U_FIRST = (5, 11)
-U_ENG = "SVSS"
+QY_LAG = 2
+HEAD = (2, 5, 3, 5)
+U_FIRST = (7, 13)
+U_ENG = "VVSV"
 X_PIECES = ((0, 256), (256, 512), (512, 1024))
-LOADS = (("x", 0), ("xs", 0), ("a", 0), ("as", 0), ("b", 0), ("bs", 0), ("as", 1), ("bs", 1), ("x", 1), ("u", 0), ("x", 2), ("u", 1), ("a", 1), ("b", 1), ("u", 2), ("u", 3), ("u", 4), ("a", 2), ("b", 2), ("u", 5))
-HEAD_SPLIT = 384
-RS_HEAD = 0
-TAIL = (((20, 21), 1, 1, 2), ((22,), 1, 1, 2), ((23,), 2, 2, 2))
+LOADS = (("x", 0), ("xs", 0), ("a", 0), ("as", 0), ("b", 0), ("bs", 0), ("x", 1), ("u", 0), ("x", 2), ("u", 1), ("a", 1), ("as", 1), ("bs", 1), ("b", 1), ("u", 2), ("u", 3), ("a", 2), ("u", 4), ("b", 2), ("u", 5))
+HEAD_SPLIT = 320
+RS_HEAD = 4
+TAIL = (((20, 21), 1, 1, 1), ((22,), 1, 1, 2), ((23,), 2, 2, 2))
 LEAD = 1
 S_PIECES = ((0, CHUNK), (CHUNK, V))
-POOL_LOADS = (("bs", 0), ("as", 1), ("bs", 1))
+POOL_LOADS = ()
+ACT_TILES = (0, 2, 4, 6, 8, 10, 12, 14, 16, 18, 20, 22)
+ACT_LAG = 1
+LAST_TR = 3
+LAST_QY = 0
 WARM = 7
 
 
@@ -59,8 +63,8 @@ def program_order():
     end = ru_step[-1]
     groups = []
     for j in range(5):
-        ts = ru_step[4 * j + 3] + TR_LAG
-        groups.append(((4 * j, 4 * j + 1), ts, ts + TC_LAG, ts + QY_LAG))
+        ts = ru_step[4 * j + 3] + (TR_LAG if j < 4 else LAST_TR)
+        groups.append(((4 * j, 4 * j + 1), ts, ts + TC_LAG, ts + (QY_LAG if j < 4 else LAST_QY)))
         groups.append(((4 * j + 2, 4 * j + 3), ts, ts + TC_LAG, None))
     for tiles, ts, tcs, qs in TAIL:
         groups.append((tiles, end + ts, end + tcs, end + qs))
@@ -108,10 +112,14 @@ def program_order():
                     ops.append(("castG", v[1]))
         for m in range(TILES):
             if m < TILES - 1 and m not in POOL_TILES and ru_step[m] + CAST_LAG == n:
-                ops.append(("castV", m))
+                if m not in ACT_TILES:
+                    ops.append(("castV", m))
         for k in range(TILES):
             if max(k + RS_LAG, RS_HEAD + k // 2) == n:
                 ops.append(("rs", k))
+        for m in ACT_TILES:
+            if ru_step[m] + ACT_LAG == n:
+                ops.append(("castS", m))
         for tiles, ts, tcs, qs in groups:
             if tcs == n:
                 ops.append(("tc", tiles))
@@ -275,7 +283,7 @@ def tile_replicate_call_eqtl_t_k3_kernel(tc, x_words, x_scales, a_words, a_scale
             held["ybf", n] = t
             src = held["y", n][:].rearrange("g (p h e) -> g h p e", h=2, e=2)
             if on_pool:
-                nc.gpsimd.tensor_scalar(out=t[:], in0=src, scalar1=1.0, scalar2=-0.0, op0=ALU.mult, op1=ALU.add)
+                nc.scalar.copy(out=t[:], in_=src)
             else:
                 nc.vector.tensor_copy(out=t[:], in_=src)
 
@@ -330,7 +338,7 @@ def tile_replicate_call_eqtl_t_k3_kernel(tc, x_words, x_scales, a_words, a_scale
                     (nc.scalar if c == CHUNKS - 1 and q % 2 == 0 else nc.sync).dma_start(out=s_dst[c, 4 * q : 4 * q + 4, :], in_=ys[32 * q : 32 * q + 4, c, :].bitcast(I32))
 
         steps = {"RA": ra, "RB": rb, "RU": ru, "ca": copy_ra, "p": explained, "rs": root, "y": result, "sty": store_y,
-                 "castG": lambda n: cast(n, True), "castV": lambda n: cast(n, False), "tr": turn, "yb": result_bf16, "tc": copy_turned,
+                 "castS": lambda n: cast(n, True), "castV": lambda n: cast(n, False), "tr": turn, "yb": result_bf16, "tc": copy_turned,
                  "ui": weave_u, "qu": quant_u, "qy": quant_y, "stw": store_planes}
         for name, arg in program_order():
             steps[name](arg)

@@ -25,30 +25,30 @@ CHUNKS = V // CHUNK
 GENE_TILES = G // P
 TILES = CHUNKS * GENE_TILES
 
-FIRST_LAG = 7
-DOUBLE_STEPS = (14, 22)
-POOL_TILES = ()
-CAST_LAG = 1
+FIRST_LAG = 8
+DOUBLE_STEPS = (10, 14, 16, 18, 20, 22)
+POOL_TILES = tuple(range(23))
+CAST_LAG = 0
 P_FIRST = 0
-RS_LAG = 2
+RS_LAG = 1
 TR_LAG = 3
 TC_LAG = 0
 QY_LAG = 2
-HEAD = (2, 5, 3, 5)
-U_FIRST = (7, 13)
-U_ENG = "VVSV"
-X_PIECES = ((0, 256), (256, 512), (512, 1024))
-LOADS = (("x", 0), ("xs", 0), ("a", 0), ("as", 0), ("b", 0), ("bs", 0), ("x", 1), ("u", 0), ("x", 2), ("u", 1), ("a", 1), ("as", 1), ("bs", 1), ("b", 1), ("u", 2), ("u", 3), ("a", 2), ("u", 4), ("b", 2), ("u", 5))
-HEAD_SPLIT = 320
-RS_HEAD = 4
-TAIL = (((20, 21), 1, 1, 1), ((22,), 1, 1, 2), ((23,), 2, 2, 2))
-LEAD = 1
+HEAD = (2, 5, 4, 6)
+U_FIRST = (8, 14)
+U_ENG = "SVSV"
+X_PIECES = ((0, 384), (384, 768), (768, 1024))
+LOADS = (("a", 0), ("xs", 0), ("x", 0), ("as", 0), ("b", 0), ("bs", 0), ("x", 1), ("u", 0), ("x", 2), ("u", 1), ("a", 1), ("as", 1), ("bs", 1), ("b", 1), ("u", 2), ("u", 3), ("a", 2), ("u", 4), ("b", 2), ("u", 5))
+HEAD_SPLIT = 256
+RS_HEAD = 7
+TAIL = (((20, 21), 1, 1, 2), ((22, 23), 1, 1, 2))
+LEAD = 2
 S_PIECES = ((0, CHUNK), (CHUNK, V))
 POOL_LOADS = ()
-ACT_TILES = (0, 2, 4, 6, 8, 10, 12, 14, 16, 18, 20, 22)
+ACT_TILES = ()
 ACT_LAG = 1
 LAST_TR = 3
-LAST_QY = 0
+LAST_QY = 2
 WARM = 7
 
 
@@ -227,7 +227,8 @@ def tile_replicate_call_eqtl_t_k3_kernel(tc, x_words, x_scales, a_words, a_scale
             genes = slice(P * (n % GENE_TILES), P * (n % GENE_TILES + 1))
             k = [genes.start < hi for lo, hi in X_PIECES].index(True)
             local = slice(genes.start - X_PIECES[k][0], genes.stop - X_PIECES[k][0])
-            acc = psum.tile([P, CHUNK], F32, tag=tag, name=tag)
+            bank = "ru" if (tag, n) == ("ra", 2) else tag
+            acc = psum.tile([P, CHUNK], F32, tag=bank, name=bank)
             held[tag, n] = acc
             for g in range(PASSES):
                 nc.tensor.matmul_mx(out=acc[:], lhsT=xw[k][:, g, local].bitcast(FP8X4), lhsT_scale=xs[:, g, genes],
@@ -282,8 +283,10 @@ def tile_replicate_call_eqtl_t_k3_kernel(tc, x_words, x_scales, a_words, a_scale
             t = flow.tile([P, 2, P, 2], BF16, tag="ybf", name="ybf", bufs=12, align_bytes=64)
             held["ybf", n] = t
             src = held["y", n][:].rearrange("g (p h e) -> g h p e", h=2, e=2)
-            if on_pool:
+            if on_pool == "S":
                 nc.scalar.copy(out=t[:], in_=src)
+            elif on_pool == "G":
+                nc.gpsimd.tensor_scalar(out=t[:], in0=src, scalar1=1.0, scalar2=-0.0, op0=ALU.mult, op1=ALU.add)
             else:
                 nc.vector.tensor_copy(out=t[:], in_=src)
 
@@ -338,7 +341,7 @@ def tile_replicate_call_eqtl_t_k3_kernel(tc, x_words, x_scales, a_words, a_scale
                     (nc.scalar if c == CHUNKS - 1 and q % 2 == 0 else nc.sync).dma_start(out=s_dst[c, 4 * q : 4 * q + 4, :], in_=ys[32 * q : 32 * q + 4, c, :].bitcast(I32))
 
         steps = {"RA": ra, "RB": rb, "RU": ru, "ca": copy_ra, "p": explained, "rs": root, "y": result, "sty": store_y,
-                 "castS": lambda n: cast(n, True), "castV": lambda n: cast(n, False), "tr": turn, "yb": result_bf16, "tc": copy_turned,
+                 "castS": lambda n: cast(n, "S"), "castV": lambda n: cast(n, "V"), "castG": lambda n: cast(n, "G"), "tr": turn, "yb": result_bf16, "tc": copy_turned,
                  "ui": weave_u, "qu": quant_u, "qy": quant_y, "stw": store_planes}
         for name, arg in program_order():
             steps[name](arg)

from contextlib import ExitStack

import concourse.mybir as mybir
from concourse.masks import make_identity

S, G, V = 1024, 1024, 1536
FLOPS = 3 * 2 * S * G * V

F32 = mybir.dt.float32
BF16 = mybir.dt.bfloat16
I32 = mybir.dt.int32
U32 = mybir.dt.uint32
U8 = mybir.dt.uint8
FP8X4 = mybir.dt.float8_e4m3fn_x4
FP4X4 = mybir.dt.float4_e2m1fn_x4
ALU = mybir.AluOpType
ACT = mybir.ActivationFunctionType

P = 128
PACK = 4
K_PASS = P * PACK
PASSES = S // K_PASS
CHUNK = 512
CHUNKS = V // CHUNK
GENE_TILES = G // P
TILES = CHUNKS * GENE_TILES

FIRST_LAG = 8
DOUBLE_STEPS = (10, 14, 16, 18, 20, 22)
POOL_TILES = tuple(range(23))
CAST_LAG = 0
P_FIRST = 0
RS_LAG = 1
TR_LAG = 3
TC_LAG = 0
QY_LAG = 2
HEAD = (2, 5, 4, 6)
U_FIRST = (8, 14)
U_ENG = "SVSV"
X_PIECES = ((0, 384), (384, 768), (768, 1024))
LOADS = (("a", 0), ("xs", 0), ("x", 0), ("as", 0), ("b", 0), ("bs", 0), ("x", 1), ("u", 0), ("x", 2), ("u", 1), ("a", 1), ("as", 1), ("bs", 1), ("b", 1), ("u", 2), ("u", 3), ("a", 2), ("u", 4), ("b", 2), ("u", 5))
HEAD_SPLIT = 256
RS_HEAD = 7
TAIL = (((20, 21), 1, 1, 2), ((22, 23), 1, 1, 2))
LEAD = 2
S_PIECES = ((0, CHUNK), (CHUNK, V))
POOL_LOADS = ()
ACT_TILES = ()
ACT_LAG = 1
LAST_TR = 3
LAST_QY = 2
WARM = 7


def program_order():
    ru_step = []
    n = FIRST_LAG
    while len(ru_step) < TILES:
        ru_step.append(n)
        if n in DOUBLE_STEPS and len(ru_step) < TILES:
            ru_step.append(n)
        n += 1
    end = ru_step[-1]
    groups = []
    for j in range(5):
        ts = ru_step[4 * j + 3] + (TR_LAG if j < 4 else LAST_TR)
        groups.append(((4 * j, 4 * j + 1), ts, ts + TC_LAG, ts + (QY_LAG if j < 4 else LAST_QY)))
        groups.append(((4 * j + 2, 4 * j + 3), ts, ts + TC_LAG, None))
    for tiles, ts, tcs, qs in TAIL:
        groups.append((tiles, end + ts, end + tcs, end + qs))
    weave = {}
    quant = {}
    weave.setdefault(HEAD[0], []).append(("V", 0, 0, 0, HEAD_SPLIT))
    if HEAD_SPLIT < 512:
        weave[HEAD[0]].append(("S", 0, 0, HEAD_SPLIT, 512))
    quant.setdefault(HEAD[1], []).append((0, 0))
    weave.setdefault(HEAD[2], []).append(("V", 0, 1, 0, HEAD_SPLIT))
    if HEAD_SPLIT < 512:
        weave[HEAD[2]].append(("S", 0, 1, HEAD_SPLIT, 512))
    quant.setdefault(HEAD[3], []).append((0, 1))
    for c in (1, 2):
        for g in range(PASSES):
            for h in range(2):
                weave.setdefault(U_FIRST[c - 1] + 2 * g + h, []).append((U_ENG[2 * g + h], c, g, 256 * h, 256 * h + 256))
            quant.setdefault(U_FIRST[c - 1] + 2 * g + 2, []).append((c, g))
    ops = []
    for n in range(LEAD):
        ops += [("RA", n), ("ca", n)]
    for n in range(end + 4):
        for tiles, ts, tcs, qs in groups:
            if ts == n:
                ops.append(("tr", tiles))
        ms = [m for m in range(TILES) if ru_step[m] == n]
        for m in ms:
            ops.append(("RU", m))
        if n + LEAD < TILES:
            ops.append(("RA", n + LEAD))
        if n < TILES:
            ops.append(("RB", n))
        if n + LEAD < TILES:
            ops.append(("ca", n + LEAD))
        vs = [("y", m) for m in ms]
        if 0 <= n - 1 < TILES:
            vs = vs[:P_FIRST] + [("p", n - 1)] + vs[P_FIRST:]
        for v in vs:
            if v == ("y", TILES - 1):
                ops.append(("yb", TILES - 1))
            ops.append(v)
            if v[0] == "y":
                ops.append(("sty", v[1]))
                if v[1] in POOL_TILES:
                    ops.append(("castG", v[1]))
        for m in range(TILES):
            if m < TILES - 1 and m not in POOL_TILES and ru_step[m] + CAST_LAG == n:
                if m not in ACT_TILES:
                    ops.append(("castV", m))
        for k in range(TILES):
            if max(k + RS_LAG, RS_HEAD + k // 2) == n:
                ops.append(("rs", k))
        for m in ACT_TILES:
            if ru_step[m] + ACT_LAG == n:
                ops.append(("castS", m))
        for tiles, ts, tcs, qs in groups:
            if tcs == n:
                ops.append(("tc", tiles))
        for piece in weave.get(n, []):
            ops.append(("ui", piece))
        for q in quant.get(n, []):
            ops.append(("qu", q))
        for tiles, ts, tcs, qs in groups:
            if qs == n:
                if tiles[0] < 20:
                    tiles = tuple(range(tiles[0], tiles[0] + 4))
                ops.append(("qy", tiles))
                ops.append(("stw", tiles))
    return ops


def tile_replicate_call_eqtl_t_k3_kernel(tc, x_words, x_scales, a_words, a_scales, b_words, b_scales, u, out_0, out_1, out_2):
    nc = tc.nc
    with ExitStack() as ctx:
        keep = ctx.enter_context(tc.tile_pool(name="keep", bufs=1))
        flow = ctx.enter_context(tc.tile_pool(name="flow", bufs=4))
        psum = ctx.enter_context(tc.psum_pool(name="psum", bufs=2))
        ctx.enter_context(tc.manual_schedule())

        xw = [keep.tile([P, PASSES, hi - lo], U32, align_bytes=64, name="xw%d" % lo) for lo, hi in X_PIECES]
        aw = [keep.tile([P, PASSES, 2 * CHUNK], U8, align_bytes=64, name="aw%d" % c) for c in range(CHUNKS)]
        bw = [keep.tile([P, PASSES, CHUNK], U32, align_bytes=64, name="bw%d" % c) for c in range(CHUNKS)]
        xs = keep.tile([P, PASSES, G], U8, align_bytes=64)
        as_ = [keep.tile([P, PASSES, hi - lo], U8, align_bytes=64, name="as%d" % lo) for lo, hi in S_PIECES]
        bs = [keep.tile([P, PASSES, hi - lo], U8, align_bytes=64, name="bs%d" % lo) for lo, hi in S_PIECES]
        uraw = keep.tile([P, CHUNKS, PASSES, PACK, CHUNK], BF16, align_bytes=64)
        uweave = keep.tile([P, CHUNKS, PASSES, CHUNK, PACK], BF16, align_bytes=64)
        uw = keep.tile([P, CHUNKS, PASSES, CHUNK], U32, align_bytes=64)
        us = keep.tile([P, CHUNKS, PASSES, CHUNK], U8, align_bytes=64)
        yw = keep.tile([P, CHUNKS, G], U32, align_bytes=64)
        ys = keep.tile([P, CHUNKS, G], U8, align_bytes=64)
        yt = keep.tile([P, CHUNKS, G, PACK], BF16, align_bytes=64)
        ident = keep.tile([P, P], F32, align_bytes=64)
        first = keep.tile([P, 8], F32, align_bytes=64)

        x_src = x_words.rearrange("g p n t -> p g (n t)").bitcast(I32)
        a_src = a_words.rearrange("g p n -> p g n").bitcast(I32)
        b_src = b_words.rearrange("g p n t -> p g (n t)").bitcast(I32)
        xs_src = x_scales.rearrange("g q n -> q g n").bitcast(I32)
        as_src = a_scales.rearrange("g q n -> q g n").bitcast(I32)
        bs_src = b_scales.rearrange("g q n -> q g n").bitcast(I32)
        u_src = u.rearrange("(g p j) v -> g p j v", p=P, j=PACK)
        w_dst = out_1.rearrange("c p m t -> c p (m t)").bitcast(I32)
        s_dst = out_2.bitcast(I32)

        def load_x(k, eng=nc.sync):
            lo, hi = X_PIECES[k]
            eng.dma_start(out=xw[k][:].bitcast(I32), in_=x_src[:, :, lo:hi])

        def load_a(c, eng=nc.sync):
            eng.dma_start(out=aw[c][:].bitcast(I32), in_=a_src[:, :, 256 * c : 256 * (c + 1)])

        def load_b(c, eng=nc.sync):
            cols = slice(CHUNK * c, CHUNK * (c + 1))
            eng.dma_start(out=bw[c][:].bitcast(I32), in_=b_src[:, :, cols])

        def load_u(c, g):
            nc.sync.dma_start(out=uraw[:, c, g], in_=u_src[g, :, :, CHUNK * c : CHUNK * (c + 1)])

        nc.vector.memset(first[:], 1.0)
        nc.gpsimd.memset(xs[:].bitcast(I32), 0)
        nc.vector.memset(as_[0][:].bitcast(I32), 0)
        nc.vector.memset(bs[0][:].bitcast(I32), 0)
        if WARM:
            warm = keep.tile([P, CHUNK], BF16, align_bytes=64)
            nc.vector.memset(warm[:], 0.0)
        nc.vector.memset(as_[1][:].bitcast(I32), 0)
        nc.vector.memset(bs[1][:].bitcast(I32), 0)
        nc.scalar.activation(out=first[:, 4:8], in_=first[:, 0:4], func=ACT.Abs_reciprocal_sqrt)

        def load_scales(plane, src, row, eng=nc.sync):
            for q in range(4):
                eng.dma_start(out=plane[32 * q + row : 32 * q + row + 4].bitcast(I32), in_=src[4 * q : 4 * q + 4])

        for kind, k in LOADS:
            if kind == "x":
                load_x(k)
            elif kind == "a":
                load_a(k)
            elif kind == "b":
                load_b(k)
            elif kind == "u":
                load_u(k // 2, k % 2)
            elif kind == "xs":
                load_scales(xs, xs_src, 0)
            elif kind == "as":
                load_scales(as_[k], as_src[:, :, S_PIECES[k][0] // 4 : S_PIECES[k][1] // 4], 0, nc.gpsimd if (kind, k) in POOL_LOADS else nc.sync)
            else:
                load_scales(bs[k], bs_src[:, :, S_PIECES[k][0] // 4 : S_PIECES[k][1] // 4], 4, nc.gpsimd if (kind, k) in POOL_LOADS else nc.sync)
        make_identity(nc, ident[:])

        if WARM:
            junk = psum.tile([P, CHUNK], F32, tag="turn")
            for w in range(WARM):
                nc.tensor.matmul(out=junk[:], lhsT=warm[:, 0:P], rhs=warm[:], start=True, stop=True)

        held = {}

        def product(tag, n, rhs, rhs_scale):
            genes = slice(P * (n % GENE_TILES), P * (n % GENE_TILES + 1))
            k = [genes.start < hi for lo, hi in X_PIECES].index(True)
            local = slice(genes.start - X_PIECES[k][0], genes.stop - X_PIECES[k][0])
            bank = "ru" if (tag, n) == ("ra", 2) else tag
            acc = psum.tile([P, CHUNK], F32, tag=bank, name=bank)
            held[tag, n] = acc
            for g in range(PASSES):
                nc.tensor.matmul_mx(out=acc[:], lhsT=xw[k][:, g, local].bitcast(FP8X4), lhsT_scale=xs[:, g, genes],
                                    rhs=rhs(g), rhs_scale=rhs_scale(g), start=(g == 0), stop=(g == PASSES - 1))

        def cols_of(n):
            c = n // GENE_TILES
            return slice(CHUNK * c, CHUNK * (c + 1))

        def plane_of(planes, row, g, n):
            c = n // GENE_TILES
            k = min(c, 1)
            lo = CHUNK * c - S_PIECES[k][0]
            return planes[k][row:, g, lo : lo + CHUNK]

        def ra(n):
            c = n // GENE_TILES
            product("ra", n, lambda g: aw[c][:, g, :].bitcast(FP4X4), lambda g: plane_of(as_, 0, g, n))

        def rb(n):
            product("rb", n, lambda g: bw[n // GENE_TILES][:, g, :].bitcast(FP8X4), lambda g: plane_of(bs, 4, g, n))

        def ru(n):
            c = n // GENE_TILES
            product("ru", n, lambda g: uw[:, c, g].bitcast(FP8X4), lambda g: us[:, c, g])

        def copy_ra(n):
            t = flow.tile([P, CHUNK], F32, tag="ra_sb", name="ra_sb", bufs=LEAD + 3)
            held["ra_sb", n] = t
            nc.scalar.copy(out=t[:], in_=held["ra", n][:])

        def explained(n):
            t = flow.tile([P, CHUNK], F32, tag="prod", name="prod", bufs=8)
            held["prod", n] = t
            nc.vector.tensor_tensor(out=t[:], in0=held["rb", n][:], in1=held["ra_sb", n][:], op=ALU.mult)

        def root(n):
            t = flow.tile([P, CHUNK], F32, tag="root", name="root", bufs=FIRST_LAG + 1)
            held["root", n] = t
            nc.scalar.activation(out=t[:], in_=held["prod", n][:], func=ACT.Abs_reciprocal_sqrt, scale=-1.0, bias=1.0)

        def result(n):
            t = flow.tile([P, CHUNK], F32, tag="y", name="y", bufs=8)
            held["y", n] = t
            nc.vector.tensor_tensor(out=t[:], in0=held["ru", n][:], in1=held["root", n][:], op=ALU.mult)

        def store_y(n):
            i = n % GENE_TILES
            nc.sync.dma_start(out=out_0[P * i : P * (i + 1), cols_of(n)], in_=held["y", n][:])

        def cast(n, on_pool):
            t = flow.tile([P, 2, P, 2], BF16, tag="ybf", name="ybf", bufs=12, align_bytes=64)
            held["ybf", n] = t
            src = held["y", n][:].rearrange("g (p h e) -> g h p e", h=2, e=2)
            if on_pool == "S":
                nc.scalar.copy(out=t[:], in_=src)
            elif on_pool == "G":
                nc.gpsimd.tensor_scalar(out=t[:], in0=src, scalar1=1.0, scalar2=-0.0, op0=ALU.mult, op1=ALU.add)
            else:
                nc.vector.tensor_copy(out=t[:], in_=src)

        def result_bf16(n):
            t = flow.tile([P, 2, P, 2], BF16, tag="ybf", name="ybf", bufs=12, align_bytes=64)
            held["ybf", n] = t
            order = "g (p h e) -> g h p e"
            nc.vector.tensor_tensor(out=t[:], in0=held["ru", n][:].rearrange(order, h=2, e=2),
                                    in1=held["root", n][:].rearrange(order, h=2, e=2), op=ALU.mult)

        def turn(tiles):
            bank = psum.tile([P, 2, 2, P], F32, tag="turn", name="turn")
            held["turn", tiles] = bank
            for a, n in enumerate(tiles):
                words = held["ybf", n][:].rearrange("g h p e -> g h (p e)").bitcast(F32)
                for h in range(2):
                    nc.tensor.transpose(out=bank[:, a, h, :], in_=words[:, h, :], identity=ident[:])

        def genes_of(tiles):
            lo = P * (tiles[0] % GENE_TILES)
            return slice(lo, lo + P * len(tiles))

        def copy_turned(tiles):
            c = tiles[0] // GENE_TILES
            dst = yt[:, c, genes_of(tiles), :].bitcast(F32).rearrange("p (a g) h -> p a g h", g=P)
            nc.scalar.copy(out=dst, in_=held["turn", tiles][:, 0 : len(tiles)].rearrange("p a h g -> p a g h"))

        def weave_u(piece):
            eng, c, g, lo, hi = piece
            dst = uweave[:, c, g, lo:hi, :].rearrange("p (w i) j -> p w j i", i=4)
            src = uraw[:, c, g, :, lo:hi].rearrange("p j (w i) -> p w j i", i=4)
            if eng == "V":
                nc.vector.tensor_copy(out=dst, in_=src)
            else:
                nc.scalar.copy(out=dst, in_=src)

        def quant_u(cg):
            c, g = cg
            nc.vector.quantize_mx(out=uw[:, c, g].bitcast(FP8X4), scales=us[:, c, g], in_=uweave[:, c, g].rearrange("p w j -> p (w j)"))

        def quant_y(tiles):
            c = tiles[0] // GENE_TILES
            genes = genes_of(tiles)
            nc.vector.quantize_mx(out=yw[:, c, genes].bitcast(FP8X4), scales=ys[:, c, genes], in_=yt[:, c, genes, :].rearrange("p g t -> p (g t)"))

        def store_planes(tiles):
            c = tiles[0] // GENE_TILES
            genes = genes_of(tiles)
            nc.sync.dma_start(out=w_dst[c, :, genes], in_=yw[:, c, genes].bitcast(I32))
            if tiles[-1] % GENE_TILES == GENE_TILES - 1:
                for q in range(4):
                    (nc.scalar if c == CHUNKS - 1 and q % 2 == 0 else nc.sync).dma_start(out=s_dst[c, 4 * q : 4 * q + 4, :], in_=ys[32 * q : 32 * q + 4, c, :].bitcast(I32))

        steps = {"RA": ra, "RB": rb, "RU": ru, "ca": copy_ra, "p": explained, "rs": root, "y": result, "sty": store_y,
                 "castS": lambda n: cast(n, "S"), "castV": lambda n: cast(n, "V"), "castG": lambda n: cast(n, "G"), "tr": turn, "yb": result_bf16, "tc": copy_turned,
                 "ui": weave_u, "qu": quant_u, "qy": quant_y, "stw": store_planes}
        for name, arg in program_order():
            steps[name](arg)
